import numpy as np
import ml_dtypes


def mxq(x, axis, fmt="e4m3"):
    dtype, down = {"e4m3": (ml_dtypes.float8_e4m3fn, 7), "e5m2": (ml_dtypes.float8_e5m2, 14)}[fmt]
    v = np.moveaxis(np.asarray(x, np.float32).astype(ml_dtypes.bfloat16).astype(np.float64), axis, -1)
    blocks = v.reshape(v.shape[:-1] + (-1, 32))
    amax = np.abs(blocks).max(-1, keepdims=True)
    byte = np.maximum(np.where(amax > 0, np.frexp(amax)[1] - 1 + 127, 0) - down, 1)
    scale = np.exp2(byte - 127.0)
    codes = (blocks / scale).astype(np.float32).astype(dtype).astype(np.float64)
    return np.moveaxis((codes * scale).reshape(v.shape), -1, axis)


WIDE = False


def mx_kscale(k):
    if not WIDE:
        return np.ones(k)
    levels = np.array([10, -10, 5, -5, 0])
    if k % 512:
        return np.exp2(np.random.permutation(np.resize(levels, k // 32))).repeat(32)
    a = np.empty((k // 512, 16))
    for p in range(k // 512):
        a[p, :8] = np.random.permutation(np.resize(levels, 8))
        for g in range(8):
            far = levels[np.abs(levels - a[p, g]) >= 10]
            a[p, g + 8] = far[np.random.randint(len(far))]
    return np.exp2(a.ravel()).repeat(32)


BF16 = ml_dtypes.bfloat16


def bf(x):
    return np.asarray(x, np.float32).astype(BF16)


def f64(x):
    return np.asarray(x).astype(np.float64)


E2M1 = np.array([0.0, 0.5, 1.0, 1.5, 2.0, 3.0, 4.0, 6.0, -0.0, -0.5, -1.0, -1.5, -2.0, -3.0, -4.0, -6.0])


def pack_weight(w, fmt):
    k, n = w.shape
    w = f64(bf(w)).reshape(k // 32, 32, n)
    amax = np.abs(w).max(1)
    if fmt == "e4m3":
        byte = np.frexp(amax)[1] - 1 + 127 - 7
    else:
        mant, ex = np.frexp(amax / 6.0)
        byte = np.where(mant > 0.5, ex, ex - 1) + 127
    byte = np.clip(np.where(amax > 0, byte, 1), 1, 254)
    scaled = (w * np.exp2(127.0 - byte)[:, None, :]).reshape(k, n).astype(np.float32)
    by_word = np.ascontiguousarray(scaled.reshape(k // 512, 128, 4, n).transpose(0, 1, 3, 2))
    if fmt == "e4m3":
        words = by_word.astype(ml_dtypes.float8_e4m3fn).view(np.uint8)
    else:
        c = by_word.astype(ml_dtypes.float4_e2m1fn).view(np.uint8) & 0xF
        words = c[..., 0::2] | (c[..., 1::2] << 4)
    return np.ascontiguousarray(words), np.ascontiguousarray(byte.astype(np.uint8).reshape(k // 512, 16, n))


def unpack_weight(words, scales, fmt):
    g, p, n, _ = words.shape
    if fmt == "e4m3":
        vals = np.ascontiguousarray(words).view(ml_dtypes.float8_e4m3fn).astype(np.float64)
    else:
        nib = np.empty((g, p, n, 4), np.uint8)
        nib[..., 0::2] = words & 0xF
        nib[..., 1::2] = words >> 4
        vals = E2M1[nib]
    vals = vals * np.repeat(np.exp2(scales.astype(np.float64) - 127.0), 8, axis=1)[..., None]
    return vals.transpose(0, 1, 3, 2).reshape(g * 512, n)
def pack4(w):
    words, scales = pack_weight(w, "e2m1")
    return words.reshape(words.shape[0], 128, -1), scales


def unpack4(words, scales):
    return unpack_weight(words.reshape(words.shape[0], 128, -1, 2), scales, "e2m1")


def planes(Y):
    n, m = Y.shape
    b = f64(bf(Y)).reshape(n // 32, 32, m)
    amax = np.abs(b).max(1)
    byte = np.clip(np.where(amax > 0, np.frexp(amax)[1] - 1 + 127 - 7, 1), 1, 254)
    codes = (b * np.exp2(127.0 - byte)[:, None, :]).reshape(n, m).astype(np.float32).astype(ml_dtypes.float8_e4m3fn).view(np.uint8)
    words = codes.reshape(n // 512, 128, 4, m).transpose(0, 1, 3, 2)
    return np.ascontiguousarray(words), np.ascontiguousarray(byte.astype(np.uint8).reshape(n // 512, 16, m))


SCEN, P, B, V = 5, 256, 1024, 1536


def setup_inputs():
    s = mx_kscale(B)
    t = mx_kscale(V)
    D = np.exp(1.6 * np.random.randn(1, B, V) + 0.4 * np.random.randn(SCEN, B, V))
    D = D * np.exp(0.5 * np.random.randn(V)) / (4.0 * B)
    w = np.exp(0.5 * np.random.randn(V))
    l = 0.6 + 0.8 * np.random.rand(V)
    x = np.exp(0.8 * np.random.randn(P, B) + 0.3 * np.random.randn(P, 1))
    fwd = D * (2.0 * w * t) / s[:, None]
    back = (D / t).transpose(0, 2, 1)
    fwd_words, fwd_scales = pack4(fwd.reshape(SCEN * B, V))
    back_words, back_scales = pack4(back.reshape(SCEN * V, B))
    return {"x": bf(x * s),
            "fwd_words": fwd_words, "fwd_scales": fwd_scales,
            "wlimit": bf(2.0 * w * l * t),
            "back_words": back_words, "back_scales": back_scales,
            "cost": bf(np.exp(0.3 * np.random.randn(B))),
            "step": bf(0.4 * np.exp(0.8 * np.random.randn(B)))}

def reference(x, fwd_words, fwd_scales, wlimit, back_words, back_scales, cost, step):
    F = unpack4(fwd_words, fwd_scales).reshape(SCEN, B, V)
    R = unpack4(back_words, back_scales).reshape(SCEN, V, B)
    dose = mxq(f64(x), 1, "e4m3") @ F
    over = np.maximum(dose - f64(wlimit), 0.0)
    grad = mxq(over, 2, "e4m3") @ R
    y = (grad + f64(cost)) * f64(step)
    Y = y.reshape(SCEN * P, B).T
    words, scales = planes(Y)
    return y, words, scales

@@ -1,0 +1,296 @@
+from contextlib import ExitStack
+
+import concourse.mybir as mybir
+from concourse.masks import make_identity
+
+SCEN, PLANS, BEAMS, VOXELS = 5, 256, 1024, 1536
+FLOPS = 2 * 2 * SCEN * PLANS * BEAMS * VOXELS
+
+F32 = mybir.dt.float32
+BF16 = mybir.dt.bfloat16
+I32 = mybir.dt.int32
+U32 = mybir.dt.uint32
+U8 = mybir.dt.uint8
+FP8X4 = mybir.dt.float8_e4m3fn_x4
+FP4X4 = mybir.dt.float4_e2m1fn_x4
+ALU = mybir.AluOpType
+ACT = mybir.ActivationFunctionType
+
+P = 128
+KP = 512
+GB = BEAMS // KP
+GV = VOXELS // KP
+HALVES = PLANS // P
+NT = SCEN * HALVES
+LAG_TURN = 1
+LAG_BACK = 4
+STEP_ON_VECTOR_FROM = 6
+
+
+def tile_overdose_gradient_scenarios_k7_kernel(
+    tc, x, fwd_words, fwd_scales, wlimit, back_words, back_scales, cost, step, out_0, out_1, out_2
+):
+    nc = tc.nc
+    with ExitStack() as ctx:
+        keep = ctx.enter_context(tc.tile_pool(name="keep", bufs=1))
+        ring = ctx.enter_context(tc.tile_pool(name="ring", bufs=1))
+        psum = ctx.enter_context(tc.psum_pool(name="psum", bufs=1))
+        ctx.enter_context(tc.manual_schedule())
+
+        def bank(tag):
+            return psum.tile([P, KP], F32, name=tag, tag=tag)
+
+        ident = keep.tile([P, P], F32, name="ident")
+        make_identity(nc, ident[:])
+
+        fw = [keep.tile([P, GB, 2 * VOXELS], U8, name="fw%d" % c, align_bytes=256) for c in range(SCEN)]
+        fs = [keep.tile([P, GB, VOXELS], U8, name="fs%d" % c, align_bytes=256) for c in range(SCEN)]
+        rw = [keep.tile([P, GV, 2 * BEAMS], U8, name="rw%d" % c, align_bytes=256) for c in range(SCEN)]
+        rs = [keep.tile([P, GV, BEAMS], U8, name="rs%d" % c, align_bytes=256) for c in range(SCEN)]
+        x_rows = [keep.tile([P, BEAMS], BF16, name="x_rows%d" % h) for h in range(HALVES)]
+        x_codes = [keep.tile([P, GB, P], U32, name="x_codes%d" % h, align_bytes=256) for h in range(HALVES)]
+        x_scales = [keep.tile([P, GB, P], U8, name="x_scales%d" % h, align_bytes=256) for h in range(HALVES)]
+        wl_cols = keep.tile([P, GV, 16], BF16, name="wl_cols")
+        cost_cols = keep.tile([P, 8], BF16, name="cost_cols")
+        step_cols = keep.tile([P, 8], BF16, name="step_cols")
+        wl_all = keep.tile([P, VOXELS], BF16, name="wl_all")
+        cost_all = keep.tile([P, BEAMS], F32, name="cost_all")
+        step_all = keep.tile([P, BEAMS], F32, name="step_all")
+        y_codes = keep.tile([P, GB, NT * P], U32, name="y_codes", align_bytes=256)
+        y_scales = keep.tile([P, GB, NT * P], U8, name="y_scales", align_bytes=256)
+        y = [keep.tile([P, BEAMS], F32, name="y%d" % i) for i in range(NT)]
+
+        def load_scales(plane, rows, groups, c):
+            for r in range(4):
+                nc.sync.dma_start(
+                    out=plane[:].bitcast(I32)[r:P:32, :, :],
+                    in_=rows.bitcast(I32)[groups * c : groups * (c + 1), r:16:4, :].rearrange("g q n -> q g n"),
+                )
+
+        def load_words(tile, words, groups, c, parts):
+            width = words.shape[2] // 4 // parts
+            for j in range(parts):
+                cols = slice(j * width, (j + 1) * width)
+                nc.sync.dma_start(
+                    out=tile[:].bitcast(I32)[:, :, cols],
+                    in_=words.bitcast(I32)[groups * c : groups * (c + 1), :, cols].rearrange("g p n -> p g n"),
+                )
+
+        for plane in [fs[0], fs[1], rs[0], fs[2], rs[1]]:
+            nc.vector.memset(plane[:].bitcast(I32), 0)
+
+        nc.scalar.dma_start(out=wl_cols[:, :, 0:4], in_=wlimit.rearrange("(g p t) -> p g t", p=P, t=4))
+        nc.scalar.dma_start(out=cost_cols[:], in_=cost.rearrange("(p j) -> p j", p=P))
+        nc.scalar.dma_start(out=step_cols[:], in_=step.rearrange("(p j) -> p j", p=P))
+        for h in range(HALVES):
+            nc.sync.dma_start(out=x_rows[h][:], in_=x[h * P : (h + 1) * P, :])
+        load_scales(fs[0], fwd_scales, GB, 0)
+        load_words(fw[0], fwd_words, GB, 0, GV)
+        load_scales(fs[1], fwd_scales, GB, 1)
+        load_words(fw[1], fwd_words, GB, 1, 1)
+        load_scales(rs[0], back_scales, GV, 0)
+        load_words(rw[0], back_words, GV, 0, 1)
+
+        def turn_x(h, tag):
+            turned = bank(tag)
+            words = x_rows[h][:].bitcast(F32)
+            for g in range(GB):
+                for u in range(2):
+                    s = 2 * g + u
+                    nc.tensor.transpose(
+                        turned[:, s * P : (s + 1) * P], words[:, 256 * g + u : 256 * (g + 1) : 2], ident[:]
+                    )
+            grouped = ring.tile([P, BEAMS], BF16, name="x_grouped", tag="x_grouped", bufs=2, align_bytes=256)
+            nc.scalar.copy(
+                out=grouped[:].bitcast(F32).rearrange("p (g r u) -> p g r u", g=GB, u=2),
+                in_=turned[:].rearrange("p (g u r) -> p g r u", g=GB, u=2),
+            )
+            nc.vector.quantize_mx(
+                out=x_codes[h][:].rearrange("p g r -> p (g r)").bitcast(FP8X4),
+                scales=x_scales[h][:].rearrange("p g r -> p (g r)"),
+                in_=grouped[:],
+            )
+
+        def spread(turned, s, column):
+            nc.tensor.transpose(turned[:, s * P : (s + 1) * P], column.to_broadcast([P, P]), ident[:])
+
+        def spread_wlimit():
+            words = wl_cols[:].bitcast(F32)
+            for tag, groups in (("turn_a", (0, 1)), ("turn_b", (2,))):
+                turned = bank(tag)
+                for g in groups:
+                    for u in range(2):
+                        spread(turned, 2 * (g - groups[0]) + u, words[:, g, u : u + 1])
+                n = 256 * len(groups)
+                nc.scalar.copy(
+                    out=wl_all[:].bitcast(F32)[:, 256 * groups[0] : 256 * groups[0] + n], in_=turned[:, 0:n]
+                )
+
+        def spread_row(cols, full, tag):
+            turned = bank(tag)
+            words = cols[:].bitcast(F32)
+            for j in range(4):
+                spread(turned, j, words[:, j : j + 1])
+            nc.scalar.copy(
+                out=full[:].rearrange("m (p j e) -> m p j e", j=4, e=2),
+                in_=turned[:].bitcast(BF16).rearrange("m (j p e) -> m p j e", j=4, e=2),
+            )
+
+        over_rows, over_turned, over_grouped, over_codes, over_scales = {}, {}, {}, {}, {}
+        y_rows, y_turned, y_grouped = {}, {}, {}
+
+        def forward(i):
+            c, h = divmod(i, HALVES)
+            over_rows[i] = ring.tile([P, VOXELS], BF16, name="over_rows", tag="over_rows", bufs=3)
+            for j in range(GV):
+                dose = bank("dose%d" % j)
+                for g in range(GB):
+                    nc.tensor.matmul_mx(
+                        out=dose[:],
+                        lhsT=x_codes[h][:, g, :].bitcast(FP8X4),
+                        lhsT_scale=x_scales[h][:, g, :],
+                        rhs=fw[c][:, g, 2 * KP * j : 2 * KP * (j + 1)].bitcast(FP4X4),
+                        rhs_scale=fs[c][:, g, KP * j : KP * (j + 1)],
+                        start=(g == 0),
+                        stop=(g == GB - 1),
+                    )
+                cols = slice(KP * j, KP * (j + 1))
+                nc.vector.tensor_tensor(
+                    out=over_rows[i][:, cols].rearrange("m (u p e) -> m u p e", u=2, e=2),
+                    in0=dose[:].rearrange("m (p u e) -> m u p e", u=2, e=2),
+                    in1=wl_all[:, cols].rearrange("m (u p e) -> m u p e", u=2, e=2),
+                    op=ALU.subtract,
+                )
+
+        def turn_over(i):
+            words = over_rows[i][:].bitcast(F32)
+            over_turned[i] = (bank("turn_a"), bank("turn_b"))
+            for s in range(2 * GV):
+                nc.tensor.transpose(
+                    over_turned[i][s // 4][:, (s % 4) * P : (s % 4 + 1) * P], words[:, s * P : (s + 1) * P], ident[:]
+                )
+
+        def group_over(i):
+            over_grouped[i] = ring.tile(
+                [P, VOXELS], BF16, name="over_grouped", tag="over_grouped", bufs=2, align_bytes=256
+            )
+            for g in range(GV):
+                half = over_turned[i][g // 2][:, 256 * (g % 2) : 256 * (g % 2 + 1)]
+                nc.scalar.activation(
+                    out=over_grouped[i][:, KP * g : KP * (g + 1)].rearrange("p (r u e) -> p r u e", u=2, e=2),
+                    in_=half.bitcast(BF16).rearrange("p (u r e) -> p r u e", u=2, e=2),
+                    func=ACT.Relu,
+                )
+
+        def quantize_over(i):
+            over_codes[i] = ring.tile([P, GV * P], U32, name="over_codes", tag="over_codes", bufs=4, align_bytes=256)
+            over_scales[i] = ring.tile([P, GV * P], U8, name="over_scales", tag="over_scales", bufs=4, align_bytes=256)
+            for lo, hi in ((0, 2), (2, 3)):
+                nc.vector.quantize_mx(
+                    out=over_codes[i][:, lo * P : hi * P].bitcast(FP8X4),
+                    scales=over_scales[i][:, lo * P : hi * P],
+                    in_=over_grouped[i][:, lo * KP : hi * KP],
+                )
+
+        def backward(i):
+            c = i // HALVES
+            sums = []
+            for n in range(GB):
+                grad = bank("grad%d" % n)
+                for g in range(GV):
+                    nc.tensor.matmul_mx(
+                        out=grad[:],
+                        lhsT=over_codes[i][:, g * P : (g + 1) * P].bitcast(FP8X4),
+                        lhsT_scale=over_scales[i][:, g * P : (g + 1) * P],
+                        rhs=rw[c][:, g, 2 * KP * n : 2 * KP * (n + 1)].bitcast(FP4X4),
+                        rhs_scale=rs[c][:, g, KP * n : KP * (n + 1)],
+                        start=(g == 0),
+                        stop=(g == GV - 1),
+                    )
+                cols = slice(KP * n, KP * (n + 1))
+                total = ring.tile([P, KP], F32, name="total", tag="total", bufs=4)
+                nc.vector.tensor_tensor(out=total[:], in0=grad[:], in1=cost_all[:, cols], op=ALU.add)
+                sums.append(total)
+                if i < STEP_ON_VECTOR_FROM:
+                    nc.gpsimd.tensor_tensor(out=y[i][:, cols], in0=total[:], in1=step_all[:, cols], op=ALU.mult)
+            if i >= STEP_ON_VECTOR_FROM:
+                for n in range(GB):
+                    cols = slice(KP * n, KP * (n + 1))
+                    nc.vector.tensor_tensor(out=y[i][:, cols], in0=sums[n][:], in1=step_all[:, cols], op=ALU.mult)
+
+        def round_y(i):
+            y_rows[i] = ring.tile([P, BEAMS], BF16, name="y_rows", tag="y_rows", bufs=2)
+            for n in range(GB):
+                cols = slice(KP * n, KP * (n + 1))
+                nc.scalar.copy(
+                    out=y_rows[i][:, cols].rearrange("m (u p e) -> m u p e", u=2, e=2),
+                    in_=y[i][:, cols].rearrange("m (p u e) -> m u p e", u=2, e=2),
+                )
+            c, h = divmod(i, HALVES)
+            nc.sync.dma_start(out=out_0[c, h * P : (h + 1) * P, :], in_=y[i][:])
+
+        def turn_y(i):
+            words = y_rows[i][:].bitcast(F32)
+            y_turned[i] = bank("turn_y")
+            for s in range(2 * GB):
+                nc.tensor.transpose(y_turned[i][:, s * P : (s + 1) * P], words[:, s * P : (s + 1) * P], ident[:])
+
+        def group_y(i):
+            y_grouped[i] = ring.tile([P, BEAMS], BF16, name="y_grouped", tag="y_grouped", bufs=2, align_bytes=256)
+            nc.scalar.copy(
+                out=y_grouped[i][:].bitcast(F32).rearrange("p (g r u) -> p g r u", g=GB, u=2),
+                in_=y_turned[i][:].rearrange("p (g u r) -> p g r u", g=GB, u=2),
+            )
+
+        def store_planes(lo, hi):
+            cols = slice(lo * P, hi * P)
+            words = out_1.rearrange("g p m t -> p g (m t)").bitcast(I32)
+            nc.sync.dma_start(out=words[:, :, cols], in_=y_codes[:].bitcast(I32)[:, :, cols])
+            quads = slice(lo * P // 4, hi * P // 4)
+            for q in range(4):
+                nc.sync.dma_start(
+                    out=out_2.bitcast(I32)[:, 4 * q : 4 * q + 4, quads].rearrange("g r n -> r g n"),
+                    in_=y_scales[:].bitcast(I32)[32 * q : 32 * q + 4, :, quads],
+                )
+
+        def quantize_y(i):
+            for g in range(GB):
+                nc.vector.quantize_mx(
+                    out=y_codes[:, g, i * P : (i + 1) * P].bitcast(FP8X4),
+                    scales=y_scales[:, g, i * P : (i + 1) * P],
+                    in_=y_grouped[i][:, g * KP : (g + 1) * KP],
+                )
+            if i in (3, 7, 9):
+                store_planes({3: 0, 7: 4, 9: 8}[i], i + 1)
+
+        turn_x(0, "turn_y")
+        spread_wlimit()
+        turn_x(1, "grad0")
+        for plane in [fs[3], rs[2], fs[4], rs[3], rs[4]]:
+            nc.vector.memset(plane[:].bitcast(I32), 0)
+        for c in range(2, SCEN + 1):
+            if c < SCEN:
+                load_scales(fs[c], fwd_scales, GB, c)
+            load_scales(rs[c - 1], back_scales, GV, c - 1)
+            if c < SCEN:
+                load_words(fw[c], fwd_words, GB, c, 1)
+            load_words(rw[c - 1], back_words, GV, c - 1, 1)
+
+
+        def run(stage, i):
+            if 0 <= i < NT:
+                stage(i)
+
+        for k in range(NT + LAG_BACK + 2):
+            run(group_y, k - LAG_BACK - 2)
+            run(group_over, k - LAG_TURN - 1)
+            run(backward, k - LAG_BACK)
+            run(forward, k)
+            run(round_y, k - LAG_BACK)
+            if k == 0:
+                spread_row(cost_cols, cost_all, "grad0")
+                spread_row(step_cols, step_all, "grad1")
+            run(turn_y, k - LAG_BACK - 1)
+            run(turn_over, k - LAG_TURN)
+            run(quantize_over, k - LAG_TURN - 1)
+            run(quantize_y, k - LAG_BACK - 2)

@@ -25,6 +25,12 @@ NT = SCEN * HALVES
 LAG_TURN = 1
 LAG_BACK = 4
 STEP_ON_VECTOR_FROM = 6
+SPLIT_FROM = 7
+FWD_RUNS = ((0, 1), (1, 2), (2, 4), (4, 5))
+BACK_RUNS = ((0, 1), (1, 3), (3, 5))
+WORD_STORES = ((0, 4), (4, 8), (8, 10))
+SCALE_STORES = ((0, 8), (8, 10))
+FREED = ("dose0", "dose1", "dose2", "turn_a", "turn_b", "turn_y")
 
 
 def tile_overdose_gradient_scenarios_k7_kernel(
@@ -42,11 +48,23 @@ def tile_overdose_gradient_scenarios_k7_kernel(
 
         ident = keep.tile([P, P], F32, name="ident")
         make_identity(nc, ident[:])
+        warm = keep.tile([P, 8], F32, name="warm")
+        nc.vector.memset(warm[:, 0:1], 0.0)
+        nc.scalar.activation(out=warm[:, 1:2], in_=warm[:, 0:1], func=ACT.Relu)
 
-        fw = [keep.tile([P, GB, 2 * VOXELS], U8, name="fw%d" % c, align_bytes=256) for c in range(SCEN)]
-        fs = [keep.tile([P, GB, VOXELS], U8, name="fs%d" % c, align_bytes=256) for c in range(SCEN)]
-        rw = [keep.tile([P, GV, 2 * BEAMS], U8, name="rw%d" % c, align_bytes=256) for c in range(SCEN)]
-        rs = [keep.tile([P, GV, BEAMS], U8, name="rs%d" % c, align_bytes=256) for c in range(SCEN)]
+        def byte_tile(name, groups, width):
+            return keep.tile([P, groups, width], U8, name=name, align_bytes=256)
+
+        fw_first = byte_tile("fw_first", GB, 2 * KP)
+        fw = [byte_tile("fw%d" % c, GB, 2 * VOXELS) for c in range(SCEN)]
+        rw = [byte_tile("rw%d" % c, GV, 2 * BEAMS) for c in range(SCEN)]
+        fs = {lo: byte_tile("fs%d" % lo, GB * (hi - lo), VOXELS) for lo, hi in FWD_RUNS}
+        rs = {lo: byte_tile("rs%d" % lo, GV * (hi - lo), BEAMS) for lo, hi in BACK_RUNS}
+
+        def scale_rows(planes, runs, groups, c, g):
+            lo = max(a for a, b in runs if a <= c)
+            return planes[lo][:, groups * (c - lo) + g, :]
+
         x_rows = [keep.tile([P, BEAMS], BF16, name="x_rows%d" % h) for h in range(HALVES)]
         x_codes = [keep.tile([P, GB, P], U32, name="x_codes%d" % h, align_bytes=256) for h in range(HALVES)]
         x_scales = [keep.tile([P, GB, P], U8, name="x_scales%d" % h, align_bytes=256) for h in range(HALVES)]
@@ -56,40 +74,62 @@ def tile_overdose_gradient_scenarios_k7_kernel(
         wl_all = keep.tile([P, VOXELS], BF16, name="wl_all")
         cost_all = keep.tile([P, BEAMS], F32, name="cost_all")
         step_all = keep.tile([P, BEAMS], F32, name="step_all")
-        y_codes = keep.tile([P, GB, NT * P], U32, name="y_codes", align_bytes=256)
-        y_scales = keep.tile([P, GB, NT * P], U8, name="y_scales", align_bytes=256)
+        y_codes = {
+            (lo, g): keep.tile([P, (hi - lo) * P], U32, name="y_codes%d_%d" % (lo, g), align_bytes=256)
+            for lo, hi in WORD_STORES
+            for g in range(GB)
+        }
+        y_scales = {lo: byte_tile("y_scales%d" % lo, GB, (hi - lo) * P) for lo, hi in SCALE_STORES}
         y = [keep.tile([P, BEAMS], F32, name="y%d" % i) for i in range(NT)]
 
-        def load_scales(plane, rows, groups, c):
+        def clear_scales(plane, groups, lo, hi):
+            nc.vector.memset(plane[lo][:].bitcast(I32), 0)
+
+        def load_scales(plane, rows, groups, lo, hi):
+            span = slice(groups * lo, groups * hi)
             for r in range(4):
                 nc.sync.dma_start(
-                    out=plane[:].bitcast(I32)[r:P:32, :, :],
-                    in_=rows.bitcast(I32)[groups * c : groups * (c + 1), r:16:4, :].rearrange("g q n -> q g n"),
+                    out=plane[lo][:].bitcast(I32)[r:P:32, :, :],
+                    in_=rows.bitcast(I32)[span, r:16:4, :].rearrange("g q n -> q g n"),
                 )
 
-        def load_words(tile, words, groups, c, parts):
-            width = words.shape[2] // 4 // parts
-            for j in range(parts):
-                cols = slice(j * width, (j + 1) * width)
-                nc.sync.dma_start(
-                    out=tile[:].bitcast(I32)[:, :, cols],
-                    in_=words.bitcast(I32)[groups * c : groups * (c + 1), :, cols].rearrange("g p n -> p g n"),
-                )
+        def load_words(tile, words, groups, c, lo, hi):
+            cols = slice(lo // 4, hi // 4)
+            nc.sync.dma_start(
+                out=tile[:].bitcast(I32)[:, :, cols],
+                in_=words.bitcast(I32)[groups * c : groups * (c + 1), :, cols].rearrange("g p n -> p g n"),
+            )
 
-        for plane in [fs[0], fs[1], rs[0], fs[2], rs[1]]:
-            nc.vector.memset(plane[:].bitcast(I32), 0)
+        def load_fwd(c):
+            load_words(fw[c], fwd_words, GB, c, 0, 2 * VOXELS)
+
+        def load_back(c):
+            load_words(rw[c], back_words, GV, c, 0, 2 * BEAMS)
+
+        clear_scales(fs, GB, 0, 1)
+        clear_scales(fs, GB, 1, 2)
+        clear_scales(rs, GV, 0, 1)
+        clear_scales(fs, GB, 2, 4)
+        clear_scales(rs, GV, 1, 3)
+        clear_scales(fs, GB, 4, 5)
 
         nc.scalar.dma_start(out=wl_cols[:, :, 0:4], in_=wlimit.rearrange("(g p t) -> p g t", p=P, t=4))
-        nc.scalar.dma_start(out=cost_cols[:], in_=cost.rearrange("(p j) -> p j", p=P))
-        nc.scalar.dma_start(out=step_cols[:], in_=step.rearrange("(p j) -> p j", p=P))
+        nc.gpsimd.dma_start(out=cost_cols[:], in_=cost.rearrange("(p j) -> p j", p=P))
+        nc.gpsimd.dma_start(out=step_cols[:], in_=step.rearrange("(p j) -> p j", p=P))
         for h in range(HALVES):
             nc.sync.dma_start(out=x_rows[h][:], in_=x[h * P : (h + 1) * P, :])
-        load_scales(fs[0], fwd_scales, GB, 0)
-        load_words(fw[0], fwd_words, GB, 0, GV)
-        load_scales(fs[1], fwd_scales, GB, 1)
-        load_words(fw[1], fwd_words, GB, 1, 1)
-        load_scales(rs[0], back_scales, GV, 0)
-        load_words(rw[0], back_words, GV, 0, 1)
+        load_scales(fs, fwd_scales, GB, 0, 1)
+        nc.sync.dma_start(
+            out=fw_first[:].bitcast(I32),
+            in_=fwd_words.bitcast(I32)[0:GB, :, 0 : 2 * KP // 4].rearrange("g p n -> p g n"),
+        )
+        load_words(fw[0], fwd_words, GB, 0, 2 * KP, 2 * VOXELS)
+        load_scales(fs, fwd_scales, GB, 1, 2)
+        load_fwd(1)
+        load_scales(rs, back_scales, GV, 0, 1)
+        load_back(0)
+        load_scales(fs, fwd_scales, GB, 2, 4)
+        load_fwd(2)
 
         def turn_x(h, tag):
             turned = bank(tag)
@@ -149,8 +189,8 @@ def tile_overdose_gradient_scenarios_k7_kernel(
                         out=dose[:],
                         lhsT=x_codes[h][:, g, :].bitcast(FP8X4),
                         lhsT_scale=x_scales[h][:, g, :],
-                        rhs=fw[c][:, g, 2 * KP * j : 2 * KP * (j + 1)].bitcast(FP4X4),
-                        rhs_scale=fs[c][:, g, KP * j : KP * (j + 1)],
+                        rhs=(fw_first if (c, j) == (0, 0) else fw[c])[:, g, 2 * KP * j : 2 * KP * (j + 1)].bitcast(FP4X4),
+                        rhs_scale=scale_rows(fs, FWD_RUNS, GB, c, g)[:, KP * j : KP * (j + 1)],
                         start=(g == 0),
                         stop=(g == GB - 1),
                     )
@@ -203,7 +243,7 @@ def tile_overdose_gradient_scenarios_k7_kernel(
                         lhsT=over_codes[i][:, g * P : (g + 1) * P].bitcast(FP8X4),
                         lhsT_scale=over_scales[i][:, g * P : (g + 1) * P],
                         rhs=rw[c][:, g, 2 * KP * n : 2 * KP * (n + 1)].bitcast(FP4X4),
-                        rhs_scale=rs[c][:, g, KP * n : KP * (n + 1)],
+                        rhs_scale=scale_rows(rs, BACK_RUNS, GV, c, g)[:, KP * n : KP * (n + 1)],
                         start=(g == 0),
                         stop=(g == GV - 1),
                     )
@@ -213,69 +253,89 @@ def tile_overdose_gradient_scenarios_k7_kernel(
                 sums.append(total)
                 if i < STEP_ON_VECTOR_FROM:
                     nc.gpsimd.tensor_tensor(out=y[i][:, cols], in0=total[:], in1=step_all[:, cols], op=ALU.mult)
+            y_rows[i] = ring.tile([P, BEAMS], BF16, name="y_rows", tag="y_rows", bufs=3)
             if i >= STEP_ON_VECTOR_FROM:
                 for n in range(GB):
                     cols = slice(KP * n, KP * (n + 1))
+                    if (i, n) == (NT - 1, GB - 1):
+                        nc.vector.tensor_tensor(
+                            out=y_rows[i][:, cols].rearrange("m (u p e) -> m u p e", u=2, e=2),
+                            in0=sums[n][:].rearrange("m (p u e) -> m u p e", u=2, e=2),
+                            in1=step_all[:, cols].rearrange("m (p u e) -> m u p e", u=2, e=2),
+                            op=ALU.mult,
+                        )
                     nc.vector.tensor_tensor(out=y[i][:, cols], in0=sums[n][:], in1=step_all[:, cols], op=ALU.mult)
 
         def round_y(i):
-            y_rows[i] = ring.tile([P, BEAMS], BF16, name="y_rows", tag="y_rows", bufs=2)
+            c, h = divmod(i, HALVES)
             for n in range(GB):
                 cols = slice(KP * n, KP * (n + 1))
-                nc.scalar.copy(
-                    out=y_rows[i][:, cols].rearrange("m (u p e) -> m u p e", u=2, e=2),
-                    in_=y[i][:, cols].rearrange("m (p u e) -> m u p e", u=2, e=2),
-                )
-            c, h = divmod(i, HALVES)
-            nc.sync.dma_start(out=out_0[c, h * P : (h + 1) * P, :], in_=y[i][:])
+                if (i, n) != (NT - 1, GB - 1):
+                    nc.scalar.copy(
+                        out=y_rows[i][:, cols].rearrange("m (u p e) -> m u p e", u=2, e=2),
+                        in_=y[i][:, cols].rearrange("m (p u e) -> m u p e", u=2, e=2),
+                    )
+                if i == NT - 1:
+                    nc.sync.dma_start(out=out_0[c, h * P : (h + 1) * P, cols], in_=y[i][:, cols])
+            if i < NT - 1:
+                nc.sync.dma_start(out=out_0[c, h * P : (h + 1) * P, :], in_=y[i][:])
 
         def turn_y(i):
             words = y_rows[i][:].bitcast(F32)
-            y_turned[i] = bank("turn_y")
+            if i < SPLIT_FROM:
+                whole = bank("turn_y")
+                y_turned[i] = [whole[:, 256 * g : 256 * (g + 1)] for g in range(GB)]
+            else:
+                y_turned[i] = [bank(FREED[GB * (i - SPLIT_FROM) + g])[:, 0:256] for g in range(GB)]
             for s in range(2 * GB):
-                nc.tensor.transpose(y_turned[i][:, s * P : (s + 1) * P], words[:, s * P : (s + 1) * P], ident[:])
+                nc.tensor.transpose(
+                    y_turned[i][s // 2][:, (s % 2) * P : (s % 2 + 1) * P], words[:, s * P : (s + 1) * P], ident[:]
+                )
 
         def group_y(i):
             y_grouped[i] = ring.tile([P, BEAMS], BF16, name="y_grouped", tag="y_grouped", bufs=2, align_bytes=256)
-            nc.scalar.copy(
-                out=y_grouped[i][:].bitcast(F32).rearrange("p (g r u) -> p g r u", g=GB, u=2),
-                in_=y_turned[i][:].rearrange("p (g u r) -> p g r u", g=GB, u=2),
-            )
+            for g in range(GB):
+                nc.scalar.copy(
+                    out=y_grouped[i][:].bitcast(F32)[:, 256 * g : 256 * (g + 1)].rearrange("p (r u) -> p r u", u=2),
+                    in_=y_turned[i][g].rearrange("p (u r) -> p r u", u=2),
+                )
 
-        def store_planes(lo, hi):
-            cols = slice(lo * P, hi * P)
-            words = out_1.rearrange("g p m t -> p g (m t)").bitcast(I32)
-            nc.sync.dma_start(out=words[:, :, cols], in_=y_codes[:].bitcast(I32)[:, :, cols])
+        def store_scales(lo, hi, queues):
             quads = slice(lo * P // 4, hi * P // 4)
             for q in range(4):
-                nc.sync.dma_start(
+                queues[q].dma_start(
                     out=out_2.bitcast(I32)[:, 4 * q : 4 * q + 4, quads].rearrange("g r n -> r g n"),
-                    in_=y_scales[:].bitcast(I32)[32 * q : 32 * q + 4, :, quads],
+                    in_=y_scales[lo][:].bitcast(I32)[32 * q : 32 * q + 4, :, :],
                 )
 
         def quantize_y(i):
+            wlo, whi = [run for run in WORD_STORES if run[0] <= i][-1]
+            slo, shi = [run for run in SCALE_STORES if run[0] <= i][-1]
             for g in range(GB):
                 nc.vector.quantize_mx(
-                    out=y_codes[:, g, i * P : (i + 1) * P].bitcast(FP8X4),
-                    scales=y_scales[:, g, i * P : (i + 1) * P],
+                    out=y_codes[wlo, g][:, (i - wlo) * P : (i - wlo + 1) * P].bitcast(FP8X4),
+                    scales=y_scales[slo][:, g, (i - slo) * P : (i - slo + 1) * P],
                     in_=y_grouped[i][:, g * KP : (g + 1) * KP],
                 )
-            if i in (3, 7, 9):
-                store_planes({3: 0, 7: 4, 9: 8}[i], i + 1)
+                if i == whi - 1:
+                    words = out_1[g].rearrange("p m t -> p (m t)").bitcast(I32)
+                    nc.sync.dma_start(out=words[:, wlo * P : whi * P], in_=y_codes[wlo, g][:].bitcast(I32))
+            if i == shi - 1:
+                store_scales(slo, shi, [nc.sync, nc.scalar, nc.sync, nc.scalar] if i == NT - 1 else [nc.sync] * 4)
 
         turn_x(0, "turn_y")
         spread_wlimit()
         turn_x(1, "grad0")
-        for plane in [fs[3], rs[2], fs[4], rs[3], rs[4]]:
-            nc.vector.memset(plane[:].bitcast(I32), 0)
-        for c in range(2, SCEN + 1):
-            if c < SCEN:
-                load_scales(fs[c], fwd_scales, GB, c)
-            load_scales(rs[c - 1], back_scales, GV, c - 1)
-            if c < SCEN:
-                load_words(fw[c], fwd_words, GB, c, 1)
-            load_words(rw[c - 1], back_words, GV, c - 1, 1)
-
+        clear_scales(rs, GV, 3, 5)
+        load_scales(rs, back_scales, GV, 1, 3)
+        load_back(1)
+        load_fwd(3)
+        load_back(2)
+        load_scales(fs, fwd_scales, GB, 4, 5)
+        load_scales(rs, back_scales, GV, 3, 5)
+        load_fwd(4)
+        load_back(3)
+        load_back(4)
 
         def run(stage, i):
             if 0 <= i < NT:
@@ -287,7 +347,7 @@ def tile_overdose_gradient_scenarios_k7_kernel(
             run(backward, k - LAG_BACK)
             run(forward, k)
             run(round_y, k - LAG_BACK)
-            if k == 0:
+            if k == 1:
                 spread_row(cost_cols, cost_all, "grad0")
                 spread_row(step_cols, step_all, "grad1")
             run(turn_y, k - LAG_BACK - 1)

from contextlib import ExitStack

import concourse.mybir as mybir
from concourse.masks import make_identity

SCEN, PLANS, BEAMS, VOXELS = 5, 256, 1024, 1536
FLOPS = 2 * 2 * SCEN * PLANS * BEAMS * VOXELS

F32 = mybir.dt.float32
BF16 = mybir.dt.bfloat16
I32 = mybir.dt.int32
U32 = mybir.dt.uint32
U8 = mybir.dt.uint8
FP8X4 = mybir.dt.float8_e4m3fn_x4
FP4X4 = mybir.dt.float4_e2m1fn_x4
ALU = mybir.AluOpType
ACT = mybir.ActivationFunctionType

P = 128
KP = 512
GB = BEAMS // KP
GV = VOXELS // KP
HALVES = PLANS // P
NT = SCEN * HALVES
LAG_TURN = 1
LAG_BACK = 4
STEP_ON_VECTOR_FROM = 6
SPLIT_FROM = 7
FWD_RUNS = ((0, 1), (1, 2), (2, 4), (4, 5))
BACK_RUNS = ((0, 1), (1, 3), (3, 5))
WORD_STORES = ((0, 4), (4, 8), (8, 10))
SCALE_STORES = ((0, 8), (8, 10))
FREED = ("dose0", "dose1", "dose2", "turn_a", "turn_b", "turn_y")


def tile_overdose_gradient_scenarios_k7_kernel(
    tc, x, fwd_words, fwd_scales, wlimit, back_words, back_scales, cost, step, out_0, out_1, out_2
):
    nc = tc.nc
    with ExitStack() as ctx:
        keep = ctx.enter_context(tc.tile_pool(name="keep", bufs=1))
        ring = ctx.enter_context(tc.tile_pool(name="ring", bufs=1))
        psum = ctx.enter_context(tc.psum_pool(name="psum", bufs=1))
        ctx.enter_context(tc.manual_schedule())

        def bank(tag):
            return psum.tile([P, KP], F32, name=tag, tag=tag)

        ident = keep.tile([P, P], F32, name="ident")
        make_identity(nc, ident[:])
        warm = keep.tile([P, 8], F32, name="warm")
        nc.vector.memset(warm[:, 0:1], 0.0)
        nc.scalar.activation(out=warm[:, 1:2], in_=warm[:, 0:1], func=ACT.Relu)

        def byte_tile(name, groups, width):
            return keep.tile([P, groups, width], U8, name=name, align_bytes=256)

        fw_first = byte_tile("fw_first", GB, 2 * KP)
        fw = [byte_tile("fw%d" % c, GB, 2 * VOXELS) for c in range(SCEN)]
        rw = [byte_tile("rw%d" % c, GV, 2 * BEAMS) for c in range(SCEN)]
        fs = {lo: byte_tile("fs%d" % lo, GB * (hi - lo), VOXELS) for lo, hi in FWD_RUNS}
        rs = {lo: byte_tile("rs%d" % lo, GV * (hi - lo), BEAMS) for lo, hi in BACK_RUNS}

        def scale_rows(planes, runs, groups, c, g):
            lo = max(a for a, b in runs if a <= c)
            return planes[lo][:, groups * (c - lo) + g, :]

        x_rows = [keep.tile([P, BEAMS], BF16, name="x_rows%d" % h) for h in range(HALVES)]
        x_codes = [keep.tile([P, GB, P], U32, name="x_codes%d" % h, align_bytes=256) for h in range(HALVES)]
        x_scales = [keep.tile([P, GB, P], U8, name="x_scales%d" % h, align_bytes=256) for h in range(HALVES)]
        wl_cols = keep.tile([P, GV, 16], BF16, name="wl_cols")
        cost_cols = keep.tile([P, 8], BF16, name="cost_cols")
        step_cols = keep.tile([P, 8], BF16, name="step_cols")
        wl_all = keep.tile([P, VOXELS], BF16, name="wl_all")
        cost_all = keep.tile([P, BEAMS], F32, name="cost_all")
        step_all = keep.tile([P, BEAMS], F32, name="step_all")
        y_codes = {
            (lo, g): keep.tile([P, (hi - lo) * P], U32, name="y_codes%d_%d" % (lo, g), align_bytes=256)
            for lo, hi in WORD_STORES
            for g in range(GB)
        }
        y_scales = {lo: byte_tile("y_scales%d" % lo, GB, (hi - lo) * P) for lo, hi in SCALE_STORES}
        y = [keep.tile([P, BEAMS], F32, name="y%d" % i) for i in range(NT)]

        def clear_scales(plane, groups, lo, hi):
            nc.vector.memset(plane[lo][:].bitcast(I32), 0)

        def load_scales(plane, rows, groups, lo, hi):
            span = slice(groups * lo, groups * hi)
            for r in range(4):
                nc.sync.dma_start(
                    out=plane[lo][:].bitcast(I32)[r:P:32, :, :],
                    in_=rows.bitcast(I32)[span, r:16:4, :].rearrange("g q n -> q g n"),
                )

        def load_words(tile, words, groups, c, lo, hi):
            cols = slice(lo // 4, hi // 4)
            nc.sync.dma_start(
                out=tile[:].bitcast(I32)[:, :, cols],
                in_=words.bitcast(I32)[groups * c : groups * (c + 1), :, cols].rearrange("g p n -> p g n"),
            )

        def load_fwd(c):
            load_words(fw[c], fwd_words, GB, c, 0, 2 * VOXELS)

        def load_back(c):
            load_words(rw[c], back_words, GV, c, 0, 2 * BEAMS)

        clear_scales(fs, GB, 0, 1)
        clear_scales(fs, GB, 1, 2)
        clear_scales(rs, GV, 0, 1)
        clear_scales(fs, GB, 2, 4)
        clear_scales(rs, GV, 1, 3)
        clear_scales(fs, GB, 4, 5)

        nc.scalar.dma_start(out=wl_cols[:, :, 0:4], in_=wlimit.rearrange("(g p t) -> p g t", p=P, t=4))
        nc.gpsimd.dma_start(out=cost_cols[:], in_=cost.rearrange("(p j) -> p j", p=P))
        nc.gpsimd.dma_start(out=step_cols[:], in_=step.rearrange("(p j) -> p j", p=P))
        for h in range(HALVES):
            nc.sync.dma_start(out=x_rows[h][:], in_=x[h * P : (h + 1) * P, :])
        load_scales(fs, fwd_scales, GB, 0, 1)
        nc.sync.dma_start(
            out=fw_first[:].bitcast(I32),
            in_=fwd_words.bitcast(I32)[0:GB, :, 0 : 2 * KP // 4].rearrange("g p n -> p g n"),
        )
        load_words(fw[0], fwd_words, GB, 0, 2 * KP, 2 * VOXELS)
        load_scales(fs, fwd_scales, GB, 1, 2)
        load_fwd(1)
        load_scales(rs, back_scales, GV, 0, 1)
        load_back(0)
        load_scales(fs, fwd_scales, GB, 2, 4)
        load_fwd(2)

        def turn_x(h, tag):
            turned = bank(tag)
            words = x_rows[h][:].bitcast(F32)
            for g in range(GB):
                for u in range(2):
                    s = 2 * g + u
                    nc.tensor.transpose(
                        turned[:, s * P : (s + 1) * P], words[:, 256 * g + u : 256 * (g + 1) : 2], ident[:]
                    )
            grouped = ring.tile([P, BEAMS], BF16, name="x_grouped", tag="x_grouped", bufs=2, align_bytes=256)
            nc.scalar.copy(
                out=grouped[:].bitcast(F32).rearrange("p (g r u) -> p g r u", g=GB, u=2),
                in_=turned[:].rearrange("p (g u r) -> p g r u", g=GB, u=2),
            )
            nc.vector.quantize_mx(
                out=x_codes[h][:].rearrange("p g r -> p (g r)").bitcast(FP8X4),
                scales=x_scales[h][:].rearrange("p g r -> p (g r)"),
                in_=grouped[:],
            )

        def spread(turned, s, column):
            nc.tensor.transpose(turned[:, s * P : (s + 1) * P], column.to_broadcast([P, P]), ident[:])

        def spread_wlimit():
            words = wl_cols[:].bitcast(F32)
            for tag, groups in (("turn_a", (0, 1)), ("turn_b", (2,))):
                turned = bank(tag)
                for g in groups:
                    for u in range(2):
                        spread(turned, 2 * (g - groups[0]) + u, words[:, g, u : u + 1])
                n = 256 * len(groups)
                nc.scalar.copy(
                    out=wl_all[:].bitcast(F32)[:, 256 * groups[0] : 256 * groups[0] + n], in_=turned[:, 0:n]
                )

        def spread_row(cols, full, tag):
            turned = bank(tag)
            words = cols[:].bitcast(F32)
            for j in range(4):
                spread(turned, j, words[:, j : j + 1])
            nc.scalar.copy(
                out=full[:].rearrange("m (p j e) -> m p j e", j=4, e=2),
                in_=turned[:].bitcast(BF16).rearrange("m (j p e) -> m p j e", j=4, e=2),
            )

        over_rows, over_turned, over_grouped, over_codes, over_scales = {}, {}, {}, {}, {}
        y_rows, y_turned, y_grouped = {}, {}, {}

        def forward(i):
            c, h = divmod(i, HALVES)
            over_rows[i] = ring.tile([P, VOXELS], BF16, name="over_rows", tag="over_rows", bufs=3)
            for j in range(GV):
                dose = bank("dose%d" % j)
                for g in range(GB):
                    nc.tensor.matmul_mx(
                        out=dose[:],
                        lhsT=x_codes[h][:, g, :].bitcast(FP8X4),
                        lhsT_scale=x_scales[h][:, g, :],
                        rhs=(fw_first if (c, j) == (0, 0) else fw[c])[:, g, 2 * KP * j : 2 * KP * (j + 1)].bitcast(FP4X4),
                        rhs_scale=scale_rows(fs, FWD_RUNS, GB, c, g)[:, KP * j : KP * (j + 1)],
                        start=(g == 0),
                        stop=(g == GB - 1),
                    )
                cols = slice(KP * j, KP * (j + 1))
                nc.vector.tensor_tensor(
                    out=over_rows[i][:, cols].rearrange("m (u p e) -> m u p e", u=2, e=2),
                    in0=dose[:].rearrange("m (p u e) -> m u p e", u=2, e=2),
                    in1=wl_all[:, cols].rearrange("m (u p e) -> m u p e", u=2, e=2),
                    op=ALU.subtract,
                )

        def turn_over(i):
            words = over_rows[i][:].bitcast(F32)
            over_turned[i] = (bank("turn_a"), bank("turn_b"))
            for s in range(2 * GV):
                nc.tensor.transpose(
                    over_turned[i][s // 4][:, (s % 4) * P : (s % 4 + 1) * P], words[:, s * P : (s + 1) * P], ident[:]
                )

        def group_over(i):
            over_grouped[i] = ring.tile(
                [P, VOXELS], BF16, name="over_grouped", tag="over_grouped", bufs=2, align_bytes=256
            )
            for g in range(GV):
                half = over_turned[i][g // 2][:, 256 * (g % 2) : 256 * (g % 2 + 1)]
                nc.scalar.activation(
                    out=over_grouped[i][:, KP * g : KP * (g + 1)].rearrange("p (r u e) -> p r u e", u=2, e=2),
                    in_=half.bitcast(BF16).rearrange("p (u r e) -> p r u e", u=2, e=2),
                    func=ACT.Relu,
                )

        def quantize_over(i):
            over_codes[i] = ring.tile([P, GV * P], U32, name="over_codes", tag="over_codes", bufs=4, align_bytes=256)
            over_scales[i] = ring.tile([P, GV * P], U8, name="over_scales", tag="over_scales", bufs=4, align_bytes=256)
            for lo, hi in ((0, 2), (2, 3)):
                nc.vector.quantize_mx(
                    out=over_codes[i][:, lo * P : hi * P].bitcast(FP8X4),
                    scales=over_scales[i][:, lo * P : hi * P],
                    in_=over_grouped[i][:, lo * KP : hi * KP],
                )

        def backward(i):
            c = i // HALVES
            sums = []
            for n in range(GB):
                grad = bank("grad%d" % n)
                for g in range(GV):
                    nc.tensor.matmul_mx(
                        out=grad[:],
                        lhsT=over_codes[i][:, g * P : (g + 1) * P].bitcast(FP8X4),
                        lhsT_scale=over_scales[i][:, g * P : (g + 1) * P],
                        rhs=rw[c][:, g, 2 * KP * n : 2 * KP * (n + 1)].bitcast(FP4X4),
                        rhs_scale=scale_rows(rs, BACK_RUNS, GV, c, g)[:, KP * n : KP * (n + 1)],
                        start=(g == 0),
                        stop=(g == GV - 1),
                    )
                cols = slice(KP * n, KP * (n + 1))
                total = ring.tile([P, KP], F32, name="total", tag="total", bufs=4)
                nc.vector.tensor_tensor(out=total[:], in0=grad[:], in1=cost_all[:, cols], op=ALU.add)
                sums.append(total)
                if i < STEP_ON_VECTOR_FROM:
                    nc.gpsimd.tensor_tensor(out=y[i][:, cols], in0=total[:], in1=step_all[:, cols], op=ALU.mult)
            y_rows[i] = ring.tile([P, BEAMS], BF16, name="y_rows", tag="y_rows", bufs=3)
            if i >= STEP_ON_VECTOR_FROM:
                for n in range(GB):
                    cols = slice(KP * n, KP * (n + 1))
                    if (i, n) == (NT - 1, GB - 1):
                        nc.vector.tensor_tensor(
                            out=y_rows[i][:, cols].rearrange("m (u p e) -> m u p e", u=2, e=2),
                            in0=sums[n][:].rearrange("m (p u e) -> m u p e", u=2, e=2),
                            in1=step_all[:, cols].rearrange("m (p u e) -> m u p e", u=2, e=2),
                            op=ALU.mult,
                        )
                    nc.vector.tensor_tensor(out=y[i][:, cols], in0=sums[n][:], in1=step_all[:, cols], op=ALU.mult)

        def round_y(i):
            c, h = divmod(i, HALVES)
            for n in range(GB):
                cols = slice(KP * n, KP * (n + 1))
                if (i, n) != (NT - 1, GB - 1):
                    nc.scalar.copy(
                        out=y_rows[i][:, cols].rearrange("m (u p e) -> m u p e", u=2, e=2),
                        in_=y[i][:, cols].rearrange("m (p u e) -> m u p e", u=2, e=2),
                    )
                if i == NT - 1:
                    nc.sync.dma_start(out=out_0[c, h * P : (h + 1) * P, cols], in_=y[i][:, cols])
            if i < NT - 1:
                nc.sync.dma_start(out=out_0[c, h * P : (h + 1) * P, :], in_=y[i][:])

        def turn_y(i):
            words = y_rows[i][:].bitcast(F32)
            if i < SPLIT_FROM:
                whole = bank("turn_y")
                y_turned[i] = [whole[:, 256 * g : 256 * (g + 1)] for g in range(GB)]
            else:
                y_turned[i] = [bank(FREED[GB * (i - SPLIT_FROM) + g])[:, 0:256] for g in range(GB)]
            for s in range(2 * GB):
                nc.tensor.transpose(
                    y_turned[i][s // 2][:, (s % 2) * P : (s % 2 + 1) * P], words[:, s * P : (s + 1) * P], ident[:]
                )

        def group_y(i):
            y_grouped[i] = ring.tile([P, BEAMS], BF16, name="y_grouped", tag="y_grouped", bufs=2, align_bytes=256)
            for g in range(GB):
                nc.scalar.copy(
                    out=y_grouped[i][:].bitcast(F32)[:, 256 * g : 256 * (g + 1)].rearrange("p (r u) -> p r u", u=2),
                    in_=y_turned[i][g].rearrange("p (u r) -> p r u", u=2),
                )

        def store_scales(lo, hi, queues):
            quads = slice(lo * P // 4, hi * P // 4)
            for q in range(4):
                queues[q].dma_start(
                    out=out_2.bitcast(I32)[:, 4 * q : 4 * q + 4, quads].rearrange("g r n -> r g n"),
                    in_=y_scales[lo][:].bitcast(I32)[32 * q : 32 * q + 4, :, :],
                )

        def quantize_y(i):
            wlo, whi = [run for run in WORD_STORES if run[0] <= i][-1]
            slo, shi = [run for run in SCALE_STORES if run[0] <= i][-1]
            for g in range(GB):
                nc.vector.quantize_mx(
                    out=y_codes[wlo, g][:, (i - wlo) * P : (i - wlo + 1) * P].bitcast(FP8X4),
                    scales=y_scales[slo][:, g, (i - slo) * P : (i - slo + 1) * P],
                    in_=y_grouped[i][:, g * KP : (g + 1) * KP],
                )
                if i == whi - 1:
                    words = out_1[g].rearrange("p m t -> p (m t)").bitcast(I32)
                    nc.sync.dma_start(out=words[:, wlo * P : whi * P], in_=y_codes[wlo, g][:].bitcast(I32))
            if i == shi - 1:
                store_scales(slo, shi, [nc.sync, nc.scalar, nc.sync, nc.scalar] if i == NT - 1 else [nc.sync] * 4)

        turn_x(0, "turn_y")
        spread_wlimit()
        turn_x(1, "grad0")
        clear_scales(rs, GV, 3, 5)
        load_scales(rs, back_scales, GV, 1, 3)
        load_back(1)
        load_fwd(3)
        load_back(2)
        load_scales(fs, fwd_scales, GB, 4, 5)
        load_scales(rs, back_scales, GV, 3, 5)
        load_fwd(4)
        load_back(3)
        load_back(4)

        def run(stage, i):
            if 0 <= i < NT:
                stage(i)

        for k in range(NT + LAG_BACK + 2):
            run(group_y, k - LAG_BACK - 2)
            run(group_over, k - LAG_TURN - 1)
            run(backward, k - LAG_BACK)
            run(forward, k)
            run(round_y, k - LAG_BACK)
            if k == 1:
                spread_row(cost_cols, cost_all, "grad0")
                spread_row(step_cols, step_all, "grad1")
            run(turn_y, k - LAG_BACK - 1)
            run(turn_over, k - LAG_TURN)
            run(quantize_over, k - LAG_TURN - 1)
            run(quantize_y, k - LAG_BACK - 2)
